import numpy as np
import ml_dtypes


def mxq(x, axis, fmt="e4m3"):
    dtype, down = {"e4m3": (ml_dtypes.float8_e4m3fn, 7), "e5m2": (ml_dtypes.float8_e5m2, 14)}[fmt]
    v = np.moveaxis(np.asarray(x, np.float32).astype(ml_dtypes.bfloat16).astype(np.float64), axis, -1)
    blocks = v.reshape(v.shape[:-1] + (-1, 32))
    amax = np.abs(blocks).max(-1, keepdims=True)
    byte = np.maximum(np.where(amax > 0, np.frexp(amax)[1] - 1 + 127, 0) - down, 1)
    scale = np.exp2(byte - 127.0)
    codes = (blocks / scale).astype(np.float32).astype(dtype).astype(np.float64)
    return np.moveaxis((codes * scale).reshape(v.shape), -1, axis)


WIDE = False


def mx_kscale(k):
    if not WIDE:
        return np.ones(k)
    levels = np.array([10, -10, 5, -5, 0])
    if k % 512:
        return np.exp2(np.random.permutation(np.resize(levels, k // 32))).repeat(32)
    a = np.empty((k // 512, 16))
    for p in range(k // 512):
        a[p, :8] = np.random.permutation(np.resize(levels, 8))
        for g in range(8):
            far = levels[np.abs(levels - a[p, g]) >= 10]
            a[p, g + 8] = far[np.random.randint(len(far))]
    return np.exp2(a.ravel()).repeat(32)


def f64(x):
    return np.asarray(x).astype(np.float64)


def striped(idx):
    return np.tile(idx.reshape(-1, 16).T, (8, 1)).astype(np.uint16)


def unstriped(offs):
    return offs[:16].T.reshape(-1).astype(np.int64)


def striped8(idx):
    return np.concatenate([x.reshape(-1, 16).T for x in idx]).astype(np.uint16)


def runs(offs, k):
    lists = np.stack([offs[16 * r : 16 * r + 16].T.reshape(-1) for r in range(8)]).astype(np.int64)
    return lists[np.arange(k) % 512 // 64]


def pack_weight(w):
    k, n = w.shape
    w = f64(np.asarray(w, np.float32).astype(ml_dtypes.bfloat16)).reshape(k // 32, 32, n)
    amax = np.abs(w).max(1)
    byte = np.clip(np.where(amax > 0, np.frexp(amax)[1] - 1 + 127 - 7, 1), 1, 254)
    scaled = (w * np.exp2(127.0 - byte)[:, None, :]).reshape(k, n).astype(np.float32)
    words = np.ascontiguousarray(scaled.reshape(k // 512, 128, 4, n).transpose(0, 1, 3, 2)).astype(ml_dtypes.float8_e4m3fn).view(np.uint8)
    return words, np.ascontiguousarray(byte.astype(np.uint8).reshape(k // 512, 16, n))


def unpack_weight(words, scales):
    g, p, n, _ = words.shape
    vals = np.ascontiguousarray(words).view(ml_dtypes.float8_e4m3fn).astype(np.float64) * np.repeat(np.exp2(scales.astype(np.float64) - 127.0), 8, axis=1)[..., None]
    return vals.transpose(0, 1, 3, 2).reshape(g * 512, n)


def relu(v):
    return np.maximum(v, 0.0)

def planes(y):
    n, m = y.shape
    v = y.astype(np.float32).astype(ml_dtypes.bfloat16).astype(np.float64).reshape(n // 32, 32, m)
    top = np.abs(v).max(1)
    byte = np.clip(np.where(top > 0, np.frexp(top)[1] - 1 + 127 - 7, 1), 1, 254)
    codes = (v * np.exp2(127.0 - byte)[:, None, :]).reshape(n, m).astype(np.float32).astype(ml_dtypes.float8_e4m3fn).view(np.uint8)
    words = codes.reshape(n // 512, 128, 4, m).transpose(0, 1, 3, 2)
    return np.ascontiguousarray(words), np.ascontiguousarray(byte.astype(np.uint8).reshape(n // 512, 16, m))


K, T, S, H, G, U = 512, 2048, 512, 512, 2048, 1024


def setup_inputs():
    n = np.random.standard_normal
    s = mx_kscale(K)[:, None]
    packed_xT = pack_weight(n((K, T)) * s)
    packed_w1 = pack_weight(n((K, H)) / np.sqrt(K) / s)
    packed_dT = pack_weight(n((K, G)) / s)
    return {
        "x_words": packed_xT[0],
        "x_scales": packed_xT[1],
        "w1_words": packed_w1[0],
        "w1_scales": packed_w1[1],
        "gs": (np.random.uniform(0.5, 1.5, (K, 1)) * s).astype(np.float32),
        "d_words": packed_dT[0],
        "d_scales": packed_dT[1],
        "mem": n((H, U)).astype(np.float32),
        "offs": striped(np.random.permutation(T)[:S]),
        "n1": striped8(np.stack([np.random.permutation(S) for _ in range(8)])),
        "n2": striped8(np.stack([np.random.permutation(S) for _ in range(8)])),
        "k1": striped8(np.random.randint(0, G, (8, H))),
        "n3": striped8(np.stack([np.random.permutation(U)[:S] for _ in range(8)])),
    }


def reference(x_words, x_scales, w1_words, w1_scales, gs, d_words, d_scales, mem, offs, n1, n2, k1, n3):
    d_k1 = unpack_weight(d_words, d_scales)[np.arange(K)[:, None], runs(k1, K)]
    xq = unpack_weight(x_words, x_scales)[:, unstriped(offs)]
    y = unpack_weight(w1_words, w1_scales).T @ xq
    pa = y - (y[np.arange(H)[:, None], runs(n1, H)])
    pb = y[np.arange(H)[:, None], runs(n2, H)] - y
    z = f64(gs) * (relu(np.minimum(pa, pb)) - (relu(-1.0 * np.maximum(pa, pb))))
    h = 0.0625 * ((d_k1.T @ mxq(z, 0, "e4m3")))
    out = f64(mem).copy()
    out[np.arange(H)[:, None], runs(n3, H)] = h
    return (out,) + planes(out)

@@ -1,0 +1,191 @@
+from contextlib import ExitStack
+
+import concourse.mybir as mybir
+
+F32 = mybir.dt.float32
+BF16 = mybir.dt.bfloat16
+I32 = mybir.dt.int32
+U32 = mybir.dt.uint32
+U16 = mybir.dt.uint16
+U8 = mybir.dt.uint8
+FP8X4 = mybir.dt.float8_e4m3fn_x4
+ALU = mybir.AluOpType
+COPY = mybir.ActivationFunctionType.Copy
+
+P = 128
+PACK = 4
+K, T, S, H, G, U = 512, 2048, 512, 512, 2048, 1024
+HALF = S // 2
+LCOLS = HALF // 16
+FLOPS = 2 * 2 * K * H * S
+
+
+def tile_picked_denseminmodpage_none_po_kernel(tc, x_words, x_scales, w1_words, w1_scales, gs, d_words, d_scales, mem, offs, n1, n2, k1, n3, out_0, out_1, out_2):
+    nc = tc.nc
+    with ExitStack() as ctx:
+        keep = ctx.enter_context(tc.tile_pool(name="keep", bufs=1))
+        psum = ctx.enter_context(tc.psum_pool(name="psum", bufs=1))
+
+        def sb(name, shape, dtype):
+            return keep.tile(shape, dtype, name=name, align_bytes=64)
+
+        def words_of(ap):
+            return ap[0].rearrange("p c t -> p (c t)").bitcast(I32)
+
+        def load_list(name, ap):
+            tile = keep.tile([P, S // 16], U16, name=name)
+            nc.sync.dma_start(tile[:], ap)
+            return tile
+
+        def load_scale_rows(tile, ap):
+            for q in range(4):
+                nc.scalar.dma_start(tile[32 * q : 32 * q + 4, :].bitcast(I32), ap[0][4 * q : 4 * q + 4, :].bitcast(I32))
+
+        def deal(dst, src):
+            nc.vector.tensor_copy(dst.rearrange("p (t m) -> p t m", t=PACK), src.rearrange("p (m t) -> p t m", t=PACK))
+
+        xs_tab = sb("xs_tab", [P, T], U8)
+        ws_raw = sb("ws_raw", [P, H], U8)
+        ds_tab = sb("ds_tab", [P, G], U8)
+        ds_plane = sb("ds_plane", [P, H], U8)
+        nc.vector.memset(xs_tab[:].bitcast(I32), 0)
+        nc.vector.memset(ws_raw[:].bitcast(I32), 0)
+        nc.gpsimd.memset(ds_tab[:].bitcast(I32), 0)
+        nc.gpsimd.memset(ds_plane[:].bitcast(I32), 0)
+
+        offs_t = load_list("offs_t", offs)
+        xw_tab = sb("xw_tab", [P, T], I32)
+        nc.sync.dma_start(xw_tab[:], words_of(x_words))
+        load_scale_rows(xs_tab, x_scales)
+        ww_raw = sb("ww_raw", [P, H], I32)
+        nc.sync.dma_start(ww_raw[:], words_of(w1_words))
+        load_scale_rows(ws_raw, w1_scales)
+        gain = sb("gain", [P, PACK], F32)
+        nc.sync.dma_start(gain[:], gs.rearrange("(p t) o -> p (t o)", t=PACK))
+        k1_t = load_list("k1_t", k1)
+        for e in range(2):
+            nc.scalar.dma_start(ds_tab[e:P:16, :].bitcast(I32), d_scales[0][e:16:2, :].bitcast(I32))
+        dw_tab = sb("dw_tab", [P, G], I32)
+        nc.sync.dma_start(dw_tab[:], words_of(d_words))
+        n1_t = load_list("n1_t", n1)
+        n2_t = load_list("n2_t", n2)
+        n3_t = load_list("n3_t", n3)
+        mem_rows = mem.rearrange("(p t) c -> p t c", t=PACK)
+        out_rows = out_0.rearrange("(p t) c -> p t c", t=PACK)
+        page = []
+        for t in range(PACK):
+            page.append(sb("page%d" % t, [P, U], F32))
+            nc.sync.dma_start(page[t][:], mem_rows[:, t, :])
+
+        neg_gain = sb("neg_gain", [P, PACK], F32)
+        nc.scalar.activation(neg_gain[:], gain[:], COPY, scale=-1.0)
+
+        xs = sb("xs", [P, S], U8)
+        nc.vector.tensor_copy(xs[:], xs_tab[:].indirect(offs_t[:]))
+        ww = sb("ww", [P, H], I32)
+        deal(ww[:], ww_raw[:])
+        xw = sb("xw", [P, S], I32)
+        nc.vector.tensor_copy(xw[:].bitcast(U32), xw_tab[:].bitcast(U32).indirect(offs_t[:]))
+        ws = sb("ws", [P, H], U8)
+        deal(ws[:], ws_raw[:])
+        y, neg_y = [], []
+        for t in range(PACK):
+            cols = slice(t * P, (t + 1) * P)
+            acc = psum.tile([P, S], F32, name="y_acc%d" % t)
+            nc.tensor.matmul_mx(acc[:], lhsT=ww[:, cols].bitcast(FP8X4), lhsT_scale=ws[:, cols], rhs=xw[:].bitcast(FP8X4), rhs_scale=xs[:], start=True, stop=True)
+            y.append(sb("y%d" % t, [P, S], F32))
+            neg_y.append(sb("neg_y%d" % t, [P, S], F32))
+            nc.scalar.activation(y[t][:], acc[:], COPY, scale=gain[:, t : t + 1])
+            nc.scalar.activation(neg_y[t][:], acc[:], COPY, scale=neg_gain[:, t : t + 1])
+
+        ds_got = sb("ds_got", [P, H], U8)
+        nc.vector.tensor_copy(ds_got[:], ds_tab[:].indirect(k1_t[:]))
+        ds_dealt = sb("ds_dealt", [P, H], U8)
+        dw_got = sb("dw_got", [P, H], I32)
+        nc.vector.tensor_copy(dw_got[:].bitcast(U32), dw_tab[:].bitcast(U32).indirect(k1_t[:]))
+        deal(ds_dealt[:], ds_got[:])
+        dw = sb("dw", [P, H], I32)
+        deal(dw[:], dw_got[:])
+        for i in range(4):
+            src = 16 * (i // 2) + i % 2
+            nc.sync.dma_start(ds_plane[i:P:32, :].bitcast(I32), ds_dealt[src:P:32, :].bitcast(I32))
+
+        def minmod(h):
+            cols = slice(h * HALF, (h + 1) * HALF)
+            lcols = slice(h * LCOLS, (h + 1) * LCOLS)
+            pa = sb("pa%d" % h, [P, PACK, HALF], F32)
+            pb = sb("pb%d" % h, [P, PACK, HALF], F32)
+            cap = sb("cap%d" % h, [P, PACK, HALF], F32)
+            z = sb("z%d" % h, [P, PACK, HALF], BF16)
+            for u in range(2):
+                for t in (2 * u, 2 * u + 1):
+                    nc.vector.tensor_tensor(pa[:, t, :], neg_y[t][:].indirect(n1_t[:, lcols]), y[t][:, cols], ALU.add)
+                    nc.vector.tensor_tensor(pb[:, t, :], y[t][:].indirect(n2_t[:, lcols]), neg_y[t][:, cols], ALU.add)
+            for u in range(2):
+                ts = slice(2 * u, 2 * u + 2)
+                nc.vector.scalar_tensor_tensor(cap[:, ts, :], pb[:, ts, :], 0.0, pa[:, ts, :], ALU.max, ALU.min)
+            for u in range(2):
+                ts = slice(2 * u, 2 * u + 2)
+                nc.vector.scalar_tensor_tensor(z[:, ts, :], pb[:, ts, :], 0.0, cap[:, ts, :], ALU.min, ALU.max)
+            zg = sb("zg%d" % h, [P, HALF, PACK], BF16)
+            nc.scalar.copy(zg[:], z[:].rearrange("p t j -> p j t"))
+            return zg
+
+        def second_product(h, zg):
+            zw = sb("zw%d" % h, [P, HALF], I32)
+            zs = sb("zs%d" % h, [P, HALF], U8)
+            nc.vector.quantize_mx(zw[:].bitcast(FP8X4), zs[:], zg[:].rearrange("p j t -> p (j t)"))
+            hs = []
+            for u in range(2):
+                acc = psum.tile([P, 2, HALF], F32, name="h_acc%d%d" % (h, u))
+                for e in range(2):
+                    t = 2 * u + e
+                    cols = slice(t * P, (t + 1) * P)
+                    nc.tensor.matmul_mx(acc[:, e, :], lhsT=dw[:, cols].bitcast(FP8X4), lhsT_scale=ds_plane[:, cols], rhs=zw[:].bitcast(FP8X4), rhs_scale=zs[:], start=True, stop=True)
+                pair = sb("h%d%d" % (h, u), [P, 2, HALF], F32)
+                nc.scalar.activation(pair[:], acc[:], COPY, scale=0.0625)
+                hs.extend([pair[:, 0, :], pair[:, 1, :]])
+            return hs
+
+        def scatter(h, t, src):
+            nc.vector.tensor_copy(page[t][:].indirect(n3_t[:, h * LCOLS : (h + 1) * LCOLS]), src)
+
+        planes = sb("planes", [P, PACK, U], BF16)
+
+        def finish(t):
+            nc.sync.dma_start(out_rows[:, t, :], page[t][:])
+            if t < PACK - 1:
+                nc.scalar.copy(planes[:, t, :], page[t][:])
+
+        zg0 = minmod(0)
+        zg1 = minmod(1)
+        h0 = second_product(0, zg0)
+        scatter(0, 0, h0[0])
+        h1 = second_product(1, zg1)
+        scatter(0, 1, h0[1])
+        scatter(1, 0, h1[0])
+        finish(0)
+        scatter(1, 1, h1[1])
+        finish(1)
+        for t in (2, 3):
+            scatter(0, t, h0[t])
+            scatter(1, t, h1[t])
+            finish(t)
+
+        ow = sb("ow", [P, U], I32)
+        osc = sb("osc", [P, U], U8)
+        out_words = words_of(out_1)
+        for c in range(2):
+            cols = slice(c * 512, (c + 1) * 512)
+            og = sb("og%d" % c, [P, 512, PACK], BF16)
+            if c == 0:
+                nc.vector.tensor_copy(planes[:, 3, cols], page[3][:, cols])
+                nc.vector.tensor_copy(og[:], planes[:, :, cols].rearrange("p t c -> p c t"))
+            else:
+                nc.scalar.copy(planes[:, 3, cols], page[3][:, cols])
+                nc.scalar.copy(og[:], planes[:, :, cols].rearrange("p t c -> p c t"))
+            nc.vector.quantize_mx(ow[:, cols].bitcast(FP8X4), osc[:, cols], og[:].rearrange("p c t -> p (c t)"))
+            nc.sync.dma_start(out_words[:, cols], ow[:, cols])
+        for q in range(4):
+            eng = nc.sync if q % 2 == 0 else nc.scalar
+            eng.dma_start(out_2[0][4 * q : 4 * q + 4, :].bitcast(I32), osc[32 * q : 32 * q + 4, :].bitcast(I32))

@@ -37,9 +37,9 @@ def tile_picked_denseminmodpage_none_po_kernel(tc, x_words, x_scales, w1_words, 
             nc.sync.dma_start(tile[:], ap)
             return tile
 
-        def load_scale_rows(tile, ap):
+        def load_scale_rows(queue, tile, ap):
             for q in range(4):
-                nc.scalar.dma_start(tile[32 * q : 32 * q + 4, :].bitcast(I32), ap[0][4 * q : 4 * q + 4, :].bitcast(I32))
+                queue.dma_start(tile[32 * q : 32 * q + 4, :].bitcast(I32), ap[0][4 * q : 4 * q + 4, :].bitcast(I32))
 
         def deal(dst, src):
             nc.vector.tensor_copy(dst.rearrange("p (t m) -> p t m", t=PACK), src.rearrange("p (m t) -> p t m", t=PACK))
@@ -50,21 +50,20 @@ def tile_picked_denseminmodpage_none_po_kernel(tc, x_words, x_scales, w1_words, 
         ds_plane = sb("ds_plane", [P, H], U8)
         nc.vector.memset(xs_tab[:].bitcast(I32), 0)
         nc.vector.memset(ws_raw[:].bitcast(I32), 0)
-        nc.gpsimd.memset(ds_tab[:].bitcast(I32), 0)
-        nc.gpsimd.memset(ds_plane[:].bitcast(I32), 0)
+        nc.vector.memset(ds_tab[:].bitcast(I32), 0)
+        nc.vector.memset(ds_plane[:].bitcast(I32), 0)
 
         offs_t = load_list("offs_t", offs)
-        xw_tab = sb("xw_tab", [P, T], I32)
-        nc.sync.dma_start(xw_tab[:], words_of(x_words))
-        load_scale_rows(xs_tab, x_scales)
         ww_raw = sb("ww_raw", [P, H], I32)
         nc.sync.dma_start(ww_raw[:], words_of(w1_words))
-        load_scale_rows(ws_raw, w1_scales)
+        load_scale_rows(nc.sync, xs_tab, x_scales)
+        xw_tab = sb("xw_tab", [P, T], I32)
+        nc.sync.dma_start(xw_tab[:], words_of(x_words))
+        load_scale_rows(nc.sync, ws_raw, w1_scales)
         gain = sb("gain", [P, PACK], F32)
         nc.sync.dma_start(gain[:], gs.rearrange("(p t) o -> p (t o)", t=PACK))
         k1_t = load_list("k1_t", k1)
-        for e in range(2):
-            nc.scalar.dma_start(ds_tab[e:P:16, :].bitcast(I32), d_scales[0][e:16:2, :].bitcast(I32))
+        nc.sync.dma_start(ds_tab[0:P:8, :].bitcast(I32), d_scales[0].bitcast(I32))
         dw_tab = sb("dw_tab", [P, G], I32)
         nc.sync.dma_start(dw_tab[:], words_of(d_words))
         n1_t = load_list("n1_t", n1)
@@ -80,10 +79,10 @@ def tile_picked_denseminmodpage_none_po_kernel(tc, x_words, x_scales, w1_words, 
         neg_gain = sb("neg_gain", [P, PACK], F32)
         nc.scalar.activation(neg_gain[:], gain[:], COPY, scale=-1.0)
 
-        xs = sb("xs", [P, S], U8)
-        nc.vector.tensor_copy(xs[:], xs_tab[:].indirect(offs_t[:]))
         ww = sb("ww", [P, H], I32)
         deal(ww[:], ww_raw[:])
+        xs = sb("xs", [P, S], U8)
+        nc.vector.tensor_copy(xs[:], xs_tab[:].indirect(offs_t[:]))
         xw = sb("xw", [P, S], I32)
         nc.vector.tensor_copy(xw[:].bitcast(U32), xw_tab[:].bitcast(U32).indirect(offs_t[:]))
         ws = sb("ws", [P, H], U8)
@@ -107,84 +106,119 @@ def tile_picked_denseminmodpage_none_po_kernel(tc, x_words, x_scales, w1_words, 
         dw = sb("dw", [P, H], I32)
         deal(dw[:], dw_got[:])
         for i in range(4):
-            src = 16 * (i // 2) + i % 2
+            src = 8 * i
             nc.sync.dma_start(ds_plane[i:P:32, :].bitcast(I32), ds_dealt[src:P:32, :].bitcast(I32))
 
-        def minmod(h):
-            cols = slice(h * HALF, (h + 1) * HALF)
-            lcols = slice(h * LCOLS, (h + 1) * LCOLS)
-            pa = sb("pa%d" % h, [P, PACK, HALF], F32)
-            pb = sb("pb%d" % h, [P, PACK, HALF], F32)
-            cap = sb("cap%d" % h, [P, PACK, HALF], F32)
-            z = sb("z%d" % h, [P, PACK, HALF], BF16)
-            for u in range(2):
-                for t in (2 * u, 2 * u + 1):
-                    nc.vector.tensor_tensor(pa[:, t, :], neg_y[t][:].indirect(n1_t[:, lcols]), y[t][:, cols], ALU.add)
-                    nc.vector.tensor_tensor(pb[:, t, :], y[t][:].indirect(n2_t[:, lcols]), neg_y[t][:, cols], ALU.add)
-            for u in range(2):
-                ts = slice(2 * u, 2 * u + 2)
-                nc.vector.scalar_tensor_tensor(cap[:, ts, :], pb[:, ts, :], 0.0, pa[:, ts, :], ALU.max, ALU.min)
-            for u in range(2):
-                ts = slice(2 * u, 2 * u + 2)
-                nc.vector.scalar_tensor_tensor(z[:, ts, :], pb[:, ts, :], 0.0, cap[:, ts, :], ALU.min, ALU.max)
+        pa = sb("pa", [P, PACK, HALF], F32)
+        pb = sb("pb", [P, PACK, HALF], F32)
+        cap = sb("cap", [P, PACK, HALF], F32)
+        zw = sb("zw", [P, S], I32)
+        zs = sb("zs", [P, S], U8)
+
+        def half(h):
+            return slice(h * HALF, (h + 1) * HALF)
+
+        def entries(h):
+            return slice(h * LCOLS, (h + 1) * LCOLS)
+
+        def look_up_a(h, t):
+            nc.vector.tensor_tensor(pa[:, t, :], neg_y[t][:].indirect(n1_t[:, entries(h)]), y[t][:, half(h)], ALU.add)
+
+        def look_up_b(h, t):
+            nc.vector.tensor_tensor(pb[:, t, :], y[t][:].indirect(n2_t[:, entries(h)]), neg_y[t][:, half(h)], ALU.add)
+
+        def clip_above():
+            nc.vector.scalar_tensor_tensor(cap[:], pb[:], 0.0, pa[:], ALU.max, ALU.min)
+
+        def clip_below_and_weave(h):
+            z = keep.tile([P, PACK, HALF], BF16, name="z%d" % h, tag="z%d" % h, align_bytes=64)
+            nc.vector.scalar_tensor_tensor(z[:], pb[:], 0.0, cap[:], ALU.min, ALU.max)
             zg = sb("zg%d" % h, [P, HALF, PACK], BF16)
             nc.scalar.copy(zg[:], z[:].rearrange("p t j -> p j t"))
             return zg
 
-        def second_product(h, zg):
-            zw = sb("zw%d" % h, [P, HALF], I32)
-            zs = sb("zs%d" % h, [P, HALF], U8)
-            nc.vector.quantize_mx(zw[:].bitcast(FP8X4), zs[:], zg[:].rearrange("p j t -> p (j t)"))
-            hs = []
-            for u in range(2):
-                acc = psum.tile([P, 2, HALF], F32, name="h_acc%d%d" % (h, u))
-                for e in range(2):
-                    t = 2 * u + e
-                    cols = slice(t * P, (t + 1) * P)
-                    nc.tensor.matmul_mx(acc[:, e, :], lhsT=dw[:, cols].bitcast(FP8X4), lhsT_scale=ds_plane[:, cols], rhs=zw[:].bitcast(FP8X4), rhs_scale=zs[:], start=True, stop=True)
-                pair = sb("h%d%d" % (h, u), [P, 2, HALF], F32)
-                nc.scalar.activation(pair[:], acc[:], COPY, scale=0.0625)
-                hs.extend([pair[:, 0, :], pair[:, 1, :]])
-            return hs
+        def quantise_z(h, zg):
+            nc.vector.quantize_mx(zw[:, half(h)].bitcast(FP8X4), zs[:, half(h)], zg[:].rearrange("p j t -> p (j t)"))
 
-        def scatter(h, t, src):
-            nc.vector.tensor_copy(page[t][:].indirect(n3_t[:, h * LCOLS : (h + 1) * LCOLS]), src)
+        def product(acc, t, cols):
+            rows = slice(t * P, (t + 1) * P)
+            nc.tensor.matmul_mx(acc, lhsT=dw[:, rows].bitcast(FP8X4), lhsT_scale=ds_plane[:, rows], rhs=zw[:, cols].bitcast(FP8X4), rhs_scale=zs[:, cols], start=True, stop=True)
 
-        planes = sb("planes", [P, PACK, U], BF16)
+        def empty(name, acc, width, tag):
+            vals = keep.tile([P, width], F32, name=name, tag=tag, align_bytes=64)
+            nc.scalar.activation(vals[:], acc, COPY, scale=0.0625)
+            return vals
+
+        def scatter(t, cols, src):
+            nc.vector.tensor_copy(page[t][:].indirect(n3_t[:, cols]), src)
+
+        planes = [sb("planes%d" % c, [P, PACK, U // 2], BF16) for c in range(2)]
+        og = [sb("og%d" % c, [P, U // 2, PACK], BF16) for c in range(2)]
 
         def finish(t):
             nc.sync.dma_start(out_rows[:, t, :], page[t][:])
-            if t < PACK - 1:
-                nc.scalar.copy(planes[:, t, :], page[t][:])
 
-        zg0 = minmod(0)
-        zg1 = minmod(1)
-        h0 = second_product(0, zg0)
-        scatter(0, 0, h0[0])
-        h1 = second_product(1, zg1)
-        scatter(0, 1, h0[1])
-        scatter(1, 0, h1[0])
-        finish(0)
-        scatter(1, 1, h1[1])
-        finish(1)
+        def round_rows(copy, c, t):
+            copy(planes[c][:, t, :], page[t][:, c * 512 : (c + 1) * 512])
+
+        def weave_pair(copy, c, u):
+            copy(og[c][:, :, 2 * u : 2 * u + 2], planes[c][:, 2 * u : 2 * u + 2, :].rearrange("p t c -> p c t"))
+
+        for t in range(PACK):
+            look_up_b(0, t)
+            look_up_a(0, t)
+        clip_above()
+        look_up_a(1, 0)
+        zg0 = clip_below_and_weave(0)
+        look_up_a(1, 1)
+        look_up_b(1, 0)
+        look_up_b(1, 1)
+        quantise_z(0, zg0)
+        acc_a = [psum.tile([P, HALF], F32, name="acc_a%d" % t) for t in range(2)]
+        for t in range(2):
+            product(acc_a[t][:], t, half(0))
+        h_a0 = empty("h_a0", acc_a[0][:], HALF, "h_a0")
         for t in (2, 3):
-            scatter(0, t, h0[t])
-            scatter(1, t, h1[t])
+            look_up_b(1, t)
+            look_up_a(1, t)
+        clip_above()
+        zg1 = clip_below_and_weave(1)
+        scatter(0, entries(0), h_a0[:])
+        h_a1 = empty("h_a1", acc_a[1][:], HALF, "z1")
+        quantise_z(1, zg1)
+        scatter(1, entries(0), h_a1[:])
+        acc_b = [psum.tile([P, HALF], F32, name="acc_b%d" % t) for t in range(2)]
+        h_b = []
+        for t in range(2):
+            product(acc_b[t][:], t, half(1))
+            h_b.append(empty("h_b%d" % t, acc_b[t][:], HALF, "h_b%d" % t))
+        h_full = {}
+        for t in (2, 3):
+            acc = psum.tile([P, S], F32, name="acc_full%d" % t, tag="y_acc%d" % t)
+            product(acc[:], t, slice(0, S))
+            h_full[t] = empty("h_full%d" % t, acc[:], S, "h_full%d" % t)
+        for t in (0, 1):
+            scatter(t, entries(1), h_b[t][:])
             finish(t)
+            for c in range(2):
+                round_rows(nc.scalar.copy, c, t)
+        weave_pair(nc.scalar.copy, 0, 0)
+        weave_pair(nc.scalar.copy, 1, 0)
+        scatter(2, slice(0, S // 16), h_full[2][:])
+        finish(2)
+        for c in range(2):
+            round_rows(nc.scalar.copy, c, 2)
+        scatter(3, slice(0, S // 16), h_full[3][:])
+        finish(3)
 
         ow = sb("ow", [P, U], I32)
         osc = sb("osc", [P, U], U8)
         out_words = words_of(out_1)
-        for c in range(2):
+        for c, copy in enumerate((nc.vector.tensor_copy, nc.scalar.copy)):
             cols = slice(c * 512, (c + 1) * 512)
-            og = sb("og%d" % c, [P, 512, PACK], BF16)
-            if c == 0:
-                nc.vector.tensor_copy(planes[:, 3, cols], page[3][:, cols])
-                nc.vector.tensor_copy(og[:], planes[:, :, cols].rearrange("p t c -> p c t"))
-            else:
-                nc.scalar.copy(planes[:, 3, cols], page[3][:, cols])
-                nc.scalar.copy(og[:], planes[:, :, cols].rearrange("p t c -> p c t"))
-            nc.vector.quantize_mx(ow[:, cols].bitcast(FP8X4), osc[:, cols], og[:].rearrange("p c t -> p (c t)"))
+            round_rows(copy, c, 3)
+            weave_pair(copy, c, 1)
+            nc.vector.quantize_mx(ow[:, cols].bitcast(FP8X4), osc[:, cols], og[c][:].rearrange("p c t -> p (c t)"))
             nc.sync.dma_start(out_words[:, cols], ow[:, cols])
         for q in range(4):
             eng = nc.sync if q % 2 == 0 else nc.scalar

@@ -11,6 +11,7 @@ U8 = mybir.dt.uint8
 FP8X4 = mybir.dt.float8_e4m3fn_x4
 ALU = mybir.AluOpType
 COPY = mybir.ActivationFunctionType.Copy
+RELU = mybir.ActivationFunctionType.Relu
 
 P = 128
 PACK = 4
@@ -44,6 +45,9 @@ def tile_picked_denseminmodpage_none_po_kernel(tc, x_words, x_scales, w1_words, 
         def deal(dst, src):
             nc.vector.tensor_copy(dst.rearrange("p (t m) -> p t m", t=PACK), src.rearrange("p (m t) -> p t m", t=PACK))
 
+        def deal_words(dst, src):
+            nc.vector.tensor_copy(dst.rearrange("p (t m) -> p m t", t=PACK), src.rearrange("p (m t) -> p m t", t=PACK))
+
         xs_tab = sb("xs_tab", [P, T], U8)
         ws_raw = sb("ws_raw", [P, H], U8)
         ds_tab = sb("ds_tab", [P, G], U8)
@@ -64,10 +68,10 @@ def tile_picked_denseminmodpage_none_po_kernel(tc, x_words, x_scales, w1_words, 
         nc.sync.dma_start(gain[:], gs.rearrange("(p t) o -> p (t o)", t=PACK))
         k1_t = load_list("k1_t", k1)
         nc.sync.dma_start(ds_tab[0:P:8, :].bitcast(I32), d_scales[0].bitcast(I32))
-        dw_tab = sb("dw_tab", [P, G], I32)
-        nc.sync.dma_start(dw_tab[:], words_of(d_words))
         n1_t = load_list("n1_t", n1)
         n2_t = load_list("n2_t", n2)
+        dw_tab = sb("dw_tab", [P, G], I32)
+        nc.sync.dma_start(dw_tab[:], words_of(d_words))
         n3_t = load_list("n3_t", n3)
         mem_rows = mem.rearrange("(p t) c -> p t c", t=PACK)
         out_rows = out_0.rearrange("(p t) c -> p t c", t=PACK)
@@ -80,22 +84,30 @@ def tile_picked_denseminmodpage_none_po_kernel(tc, x_words, x_scales, w1_words, 
         nc.scalar.activation(neg_gain[:], gain[:], COPY, scale=-1.0)
 
         ww = sb("ww", [P, H], I32)
-        deal(ww[:], ww_raw[:])
+        deal_words(ww[:], ww_raw[:])
         xs = sb("xs", [P, S], U8)
         nc.vector.tensor_copy(xs[:], xs_tab[:].indirect(offs_t[:]))
         xw = sb("xw", [P, S], I32)
         nc.vector.tensor_copy(xw[:].bitcast(U32), xw_tab[:].bitcast(U32).indirect(offs_t[:]))
         ws = sb("ws", [P, H], U8)
         deal(ws[:], ws_raw[:])
-        y, neg_y = [], []
+        def half(h):
+            return slice(h * HALF, (h + 1) * HALF)
+
+        def entries(h):
+            return slice(h * LCOLS, (h + 1) * LCOLS)
+
+        y = [sb("y%d" % h, [P, PACK, HALF], F32) for h in range(2)]
+        neg_y, y_acc = [], []
         for t in range(PACK):
             cols = slice(t * P, (t + 1) * P)
-            acc = psum.tile([P, S], F32, name="y_acc%d" % t)
-            nc.tensor.matmul_mx(acc[:], lhsT=ww[:, cols].bitcast(FP8X4), lhsT_scale=ws[:, cols], rhs=xw[:].bitcast(FP8X4), rhs_scale=xs[:], start=True, stop=True)
-            y.append(sb("y%d" % t, [P, S], F32))
+            y_acc.append(psum.tile([P, S], F32, name="y_acc%d" % t))
+            nc.tensor.matmul_mx(y_acc[t][:], lhsT=ww[:, cols].bitcast(FP8X4), lhsT_scale=ws[:, cols], rhs=xw[:].bitcast(FP8X4), rhs_scale=xs[:], start=True, stop=True)
             neg_y.append(sb("neg_y%d" % t, [P, S], F32))
-            nc.scalar.activation(y[t][:], acc[:], COPY, scale=gain[:, t : t + 1])
-            nc.scalar.activation(neg_y[t][:], acc[:], COPY, scale=neg_gain[:, t : t + 1])
+            nc.scalar.activation(neg_y[t][:], y_acc[t][:], COPY, scale=neg_gain[:, t : t + 1])
+            nc.scalar.activation(y[0][:, t, :], y_acc[t][:, half(0)], COPY, scale=gain[:, t : t + 1])
+        for t in range(PACK):
+            nc.scalar.activation(y[1][:, t, :], y_acc[t][:, half(1)], COPY, scale=gain[:, t : t + 1])
 
         ds_got = sb("ds_got", [P, H], U8)
         nc.vector.tensor_copy(ds_got[:], ds_tab[:].indirect(k1_t[:]))
@@ -104,41 +116,37 @@ def tile_picked_denseminmodpage_none_po_kernel(tc, x_words, x_scales, w1_words, 
         nc.vector.tensor_copy(dw_got[:].bitcast(U32), dw_tab[:].bitcast(U32).indirect(k1_t[:]))
         deal(ds_dealt[:], ds_got[:])
         dw = sb("dw", [P, H], I32)
-        deal(dw[:], dw_got[:])
+        deal_words(dw[:], dw_got[:])
         for i in range(4):
             src = 8 * i
             nc.sync.dma_start(ds_plane[i:P:32, :].bitcast(I32), ds_dealt[src:P:32, :].bitcast(I32))
 
-        pa = sb("pa", [P, PACK, HALF], F32)
-        pb = sb("pb", [P, PACK, HALF], F32)
-        cap = sb("cap", [P, PACK, HALF], F32)
+        pa = [sb("pa%d" % h, [P, PACK, HALF], F32) for h in range(2)]
+        neg_pb = [sb("neg_pb%d" % h, [P, PACK, HALF], F32) for h in range(2)]
         zw = sb("zw", [P, S], I32)
         zs = sb("zs", [P, S], U8)
+        WOVEN = HALF * PACK
 
-        def half(h):
-            return slice(h * HALF, (h + 1) * HALF)
+        def look_up(dst, lst, h, t):
+            nc.vector.tensor_tensor(dst[h][:, t, :], neg_y[t][:].indirect(lst[:, entries(h)]), y[h][:, t, :], ALU.add)
 
-        def entries(h):
-            return slice(h * LCOLS, (h + 1) * LCOLS)
+        def weave(name, src, func, scale):
+            dst = sb(name, [P, WOVEN], BF16)
+            nc.scalar.activation(dst[:].rearrange("p (j t) -> p j t", t=PACK), src[:].rearrange("p t j -> p j t"), func, scale=scale)
+            return dst
 
-        def look_up_a(h, t):
-            nc.vector.tensor_tensor(pa[:, t, :], neg_y[t][:].indirect(n1_t[:, entries(h)]), y[t][:, half(h)], ALU.add)
+        def bounds(h):
+            a16 = weave("a16_%d" % h, pa[h], COPY, 1.0)
+            upper = weave("upper%d" % h, pa[h], RELU, 1.0)
+            return a16, upper
 
-        def look_up_b(h, t):
-            nc.vector.tensor_tensor(pb[:, t, :], y[t][:].indirect(n2_t[:, entries(h)]), neg_y[t][:, half(h)], ALU.add)
-
-        def clip_above():
-            nc.vector.scalar_tensor_tensor(cap[:], pb[:], 0.0, pa[:], ALU.max, ALU.min)
-
-        def clip_below_and_weave(h):
-            z = keep.tile([P, PACK, HALF], BF16, name="z%d" % h, tag="z%d" % h, align_bytes=64)
-            nc.vector.scalar_tensor_tensor(z[:], pb[:], 0.0, cap[:], ALU.min, ALU.max)
-            zg = sb("zg%d" % h, [P, HALF, PACK], BF16)
-            nc.scalar.copy(zg[:], z[:].rearrange("p t j -> p j t"))
-            return zg
+        def lower_bound(h, a16):
+            lower = sb("lower%d" % h, [P, WOVEN], BF16)
+            nc.vector.tensor_scalar_min(lower[:], a16[:], 0.0)
+            return lower
 
         def quantise_z(h, zg):
-            nc.vector.quantize_mx(zw[:, half(h)].bitcast(FP8X4), zs[:, half(h)], zg[:].rearrange("p j t -> p (j t)"))
+            nc.vector.quantize_mx(zw[:, half(h)].bitcast(FP8X4), zs[:, half(h)], zg[:])
 
         def product(acc, t, cols):
             rows = slice(t * P, (t + 1) * P)
@@ -152,40 +160,54 @@ def tile_picked_denseminmodpage_none_po_kernel(tc, x_words, x_scales, w1_words, 
         def scatter(t, cols, src):
             nc.vector.tensor_copy(page[t][:].indirect(n3_t[:, cols]), src)
 
-        planes = [sb("planes%d" % c, [P, PACK, U // 2], BF16) for c in range(2)]
-        og = [sb("og%d" % c, [P, U // 2, PACK], BF16) for c in range(2)]
+        spans = (slice(0, 512), slice(512, 768), slice(768, 1024))
+        planes = [sb("planes%d" % c, [P, PACK, s.stop - s.start], BF16) for c, s in enumerate(spans)]
+        og = [sb("og%d" % c, [P, s.stop - s.start, PACK], BF16) for c, s in enumerate(spans)]
 
         def finish(t):
             nc.sync.dma_start(out_rows[:, t, :], page[t][:])
 
         def round_rows(copy, c, t):
-            copy(planes[c][:, t, :], page[t][:, c * 512 : (c + 1) * 512])
+            copy(planes[c][:, t, :], page[t][:, spans[c]])
 
         def weave_pair(copy, c, u):
             copy(og[c][:, :, 2 * u : 2 * u + 2], planes[c][:, 2 * u : 2 * u + 2, :].rearrange("p t c -> p c t"))
 
+        def round_in_place(c, t):
+            nc.scalar.copy(og[c][:, :, t], page[t][:, spans[c]])
+
+        cap = [sb("cap%d" % h, [P, WOVEN], BF16) for h in range(2)]
+        zg = [sb("zg%d" % h, [P, WOVEN], BF16) for h in range(2)]
         for t in range(PACK):
-            look_up_b(0, t)
-            look_up_a(0, t)
-        clip_above()
-        look_up_a(1, 0)
-        zg0 = clip_below_and_weave(0)
-        look_up_a(1, 1)
-        look_up_b(1, 0)
-        look_up_b(1, 1)
-        quantise_z(0, zg0)
+            look_up(pa, n1_t, 0, t)
+            look_up(neg_pb, n2_t, 0, t)
+        a16, upper = bounds(0)
+        b16 = weave("b16_0", neg_pb[0], COPY, -1.0)
+        for t in range(PACK):
+            look_up(pa, n1_t, 1, t)
+        lower = lower_bound(0, a16)
+        look_up(neg_pb, n2_t, 1, 0)
+        nc.vector.tensor_tensor(cap[0][:], b16[:], upper[:], ALU.min)
+        look_up(neg_pb, n2_t, 1, 1)
+        nc.vector.tensor_tensor(zg[0][:], cap[0][:], lower[:], ALU.max)
+        look_up(neg_pb, n2_t, 1, 2)
+        quantise_z(0, zg[0])
+        a16, upper = bounds(1)
         acc_a = [psum.tile([P, HALF], F32, name="acc_a%d" % t) for t in range(2)]
         for t in range(2):
             product(acc_a[t][:], t, half(0))
         h_a0 = empty("h_a0", acc_a[0][:], HALF, "h_a0")
-        for t in (2, 3):
-            look_up_b(1, t)
-            look_up_a(1, t)
-        clip_above()
-        zg1 = clip_below_and_weave(1)
+        look_up(neg_pb, n2_t, 1, 3)
+        b16 = weave("b16_1", neg_pb[1], COPY, -1.0)
+        lower = lower_bound(1, a16)
         scatter(0, entries(0), h_a0[:])
-        h_a1 = empty("h_a1", acc_a[1][:], HALF, "z1")
-        quantise_z(1, zg1)
+        h_a1 = empty("h_a1", acc_a[1][:], HALF, "neg_pb1")
+        pieces = (slice(0, WOVEN // 2), slice(WOVEN // 2, WOVEN))
+        for cols in pieces:
+            nc.vector.tensor_tensor(cap[1][:, cols], b16[:, cols], upper[:, cols], ALU.min)
+        for cols in pieces:
+            nc.vector.tensor_tensor(zg[1][:, cols], cap[1][:, cols], lower[:, cols], ALU.max)
+        quantise_z(1, zg[1])
         scatter(1, entries(0), h_a1[:])
         acc_b = [psum.tile([P, HALF], F32, name="acc_b%d" % t) for t in range(2)]
         h_b = []
@@ -200,26 +222,29 @@ def tile_picked_denseminmodpage_none_po_kernel(tc, x_words, x_scales, w1_words, 
         for t in (0, 1):
             scatter(t, entries(1), h_b[t][:])
             finish(t)
-            for c in range(2):
+            for c in range(3):
                 round_rows(nc.scalar.copy, c, t)
-        weave_pair(nc.scalar.copy, 0, 0)
-        weave_pair(nc.scalar.copy, 1, 0)
+        for c in range(3):
+            weave_pair(nc.scalar.copy, c, 0)
         scatter(2, slice(0, S // 16), h_full[2][:])
         finish(2)
-        for c in range(2):
-            round_rows(nc.scalar.copy, c, 2)
+        round_rows(nc.scalar.copy, 0, 2)
+        for c in (1, 2):
+            round_in_place(c, 2)
         scatter(3, slice(0, S // 16), h_full[3][:])
         finish(3)
 
         ow = sb("ow", [P, U], I32)
         osc = sb("osc", [P, U], U8)
         out_words = words_of(out_1)
-        for c, copy in enumerate((nc.vector.tensor_copy, nc.scalar.copy)):
-            cols = slice(c * 512, (c + 1) * 512)
-            round_rows(copy, c, 3)
-            weave_pair(copy, c, 1)
+        round_rows(nc.vector.tensor_copy, 0, 3)
+        weave_pair(nc.vector.tensor_copy, 0, 1)
+        for c in (1, 2):
+            round_in_place(c, 3)
+        for c in (1, 0, 2):
+            cols = spans[c]
             nc.vector.quantize_mx(ow[:, cols].bitcast(FP8X4), osc[:, cols], og[c][:].rearrange("p c t -> p (c t)"))
             nc.sync.dma_start(out_words[:, cols], ow[:, cols])
         for q in range(4):
-            eng = nc.sync if q % 2 == 0 else nc.scalar
+            eng = nc.sync if q == 3 else nc.scalar
             eng.dma_start(out_2[0][4 * q : 4 * q + 4, :].bitcast(I32), osc[32 * q : 32 * q + 4, :].bitcast(I32))

@@ -109,7 +109,7 @@ def tile_picked_denseminmodpage_none_po_kernel(tc, x_words, x_scales, w1_words, 
         for t in range(PACK):
             nc.scalar.activation(y[1][:, t, :], y_acc[t][:, half(1)], COPY, scale=gain[:, t : t + 1])
 
-        ds_got = sb("ds_got", [P, H], U8)
+        ds_got = keep.tile([P, H], U8, name="ds_got", tag="ws_raw", align_bytes=64)
         nc.vector.tensor_copy(ds_got[:], ds_tab[:].indirect(k1_t[:]))
         ds_dealt = sb("ds_dealt", [P, H], U8)
         dw_got = sb("dw_got", [P, H], I32)
@@ -145,8 +145,9 @@ def tile_picked_denseminmodpage_none_po_kernel(tc, x_words, x_scales, w1_words, 
             nc.vector.tensor_scalar_min(lower[:], a16[:], 0.0)
             return lower
 
-        def quantise_z(h, zg):
-            nc.vector.quantize_mx(zw[:, half(h)].bitcast(FP8X4), zs[:, half(h)], zg[:])
+        def quantise_z(first, woven, count):
+            cols = slice(first, first + count)
+            nc.vector.quantize_mx(zw[:, cols].bitcast(FP8X4), zs[:, cols], woven)
 
         def product(acc, t, cols):
             rows = slice(t * P, (t + 1) * P)
@@ -160,18 +161,20 @@ def tile_picked_denseminmodpage_none_po_kernel(tc, x_words, x_scales, w1_words, 
         def scatter(t, cols, src):
             nc.vector.tensor_copy(page[t][:].indirect(n3_t[:, cols]), src)
 
-        spans = (slice(0, 512), slice(512, 768), slice(768, 1024))
-        planes = [sb("planes%d" % c, [P, PACK, s.stop - s.start], BF16) for c, s in enumerate(spans)]
-        og = [sb("og%d" % c, [P, s.stop - s.start, PACK], BF16) for c, s in enumerate(spans)]
+        spans = [slice(c * 256, (c + 1) * 256) for c in range(4)]
+        planes = [sb("planes%d" % c, [P, 2, 256], BF16) for c in range(2)]
+
+        og = [sb("og%d" % c, [P, 256, PACK], BF16) for c in range(4)]
+        low = [sb("low%d" % i, [P, 2, 512], BF16) for i in range(2)]
 
         def finish(t):
             nc.sync.dma_start(out_rows[:, t, :], page[t][:])
 
         def round_rows(copy, c, t):
-            copy(planes[c][:, t, :], page[t][:, spans[c]])
+            copy(planes[c][:, t - 2, :], page[t][:, spans[c]])
 
-        def weave_pair(copy, c, u):
-            copy(og[c][:, :, 2 * u : 2 * u + 2], planes[c][:, 2 * u : 2 * u + 2, :].rearrange("p t c -> p c t"))
+        def weave_pair(c):
+            nc.vector.tensor_copy(og[c][:, :, 2:4], planes[c][:].rearrange("p t c -> p c t"))
 
         def round_in_place(c, t):
             nc.scalar.copy(og[c][:, :, t], page[t][:, spans[c]])
@@ -185,63 +188,59 @@ def tile_picked_denseminmodpage_none_po_kernel(tc, x_words, x_scales, w1_words, 
         b16 = weave("b16_0", neg_pb[0], COPY, -1.0)
         for t in range(PACK):
             look_up(pa, n1_t, 1, t)
-        lower = lower_bound(0, a16)
-        look_up(neg_pb, n2_t, 1, 0)
+        lower0 = lower_bound(0, a16)
+        a16, upper1 = bounds(1)
+        for t in range(PACK):
+            look_up(neg_pb, n2_t, 1, t)
+        b16_1 = weave("b16_1", neg_pb[1], COPY, -1.0)
         nc.vector.tensor_tensor(cap[0][:], b16[:], upper[:], ALU.min)
-        look_up(neg_pb, n2_t, 1, 1)
-        nc.vector.tensor_tensor(zg[0][:], cap[0][:], lower[:], ALU.max)
-        look_up(neg_pb, n2_t, 1, 2)
-        quantise_z(0, zg[0])
-        a16, upper = bounds(1)
+        lower1 = lower_bound(1, a16)
+        nc.vector.tensor_tensor(zg[0][:], cap[0][:], lower0[:], ALU.max)
+        pieces = (slice(0, WOVEN // 2), slice(WOVEN // 2, WOVEN))
+        nc.vector.tensor_tensor(cap[1][:, pieces[0]], b16_1[:, pieces[0]], upper1[:, pieces[0]], ALU.min)
+        quantise_z(0, zg[0][:], HALF)
         acc_a = [psum.tile([P, HALF], F32, name="acc_a%d" % t) for t in range(2)]
         for t in range(2):
             product(acc_a[t][:], t, half(0))
         h_a0 = empty("h_a0", acc_a[0][:], HALF, "h_a0")
-        look_up(neg_pb, n2_t, 1, 3)
-        b16 = weave("b16_1", neg_pb[1], COPY, -1.0)
-        lower = lower_bound(1, a16)
+        nc.vector.tensor_tensor(cap[1][:, pieces[1]], b16_1[:, pieces[1]], upper1[:, pieces[1]], ALU.min)
+        for cols in pieces:
+            nc.vector.tensor_tensor(zg[1][:, cols], cap[1][:, cols], lower1[:, cols], ALU.max)
+        for i, cols in enumerate(pieces):
+            quantise_z(HALF + i * HALF // 2, zg[1][:, cols], HALF // 2)
+        h_a1 = empty("h_a1", acc_a[1][:], HALF, "cap1")
         scatter(0, entries(0), h_a0[:])
-        h_a1 = empty("h_a1", acc_a[1][:], HALF, "neg_pb1")
-        pieces = (slice(0, WOVEN // 2), slice(WOVEN // 2, WOVEN))
-        for cols in pieces:
-            nc.vector.tensor_tensor(cap[1][:, cols], b16[:, cols], upper[:, cols], ALU.min)
-        for cols in pieces:
-            nc.vector.tensor_tensor(zg[1][:, cols], cap[1][:, cols], lower[:, cols], ALU.max)
-        quantise_z(1, zg[1])
         scatter(1, entries(0), h_a1[:])
-        acc_b = [psum.tile([P, HALF], F32, name="acc_b%d" % t) for t in range(2)]
-        h_b = []
-        for t in range(2):
-            product(acc_b[t][:], t, half(1))
-            h_b.append(empty("h_b%d" % t, acc_b[t][:], HALF, "h_b%d" % t))
-        h_full = {}
-        for t in (2, 3):
-            acc = psum.tile([P, S], F32, name="acc_full%d" % t, tag="y_acc%d" % t)
-            product(acc[:], t, slice(0, S))
-            h_full[t] = empty("h_full%d" % t, acc[:], S, "h_full%d" % t)
-        for t in (0, 1):
-            scatter(t, entries(1), h_b[t][:])
+        rest = []
+        for t in range(PACK):
+            cols = half(1) if t < 2 else slice(0, S)
+            acc = psum.tile([P, cols.stop - cols.start], F32, name="acc_rest%d" % t, tag="y_acc%d" % t)
+            product(acc[:], t, cols)
+            rest.append(empty("h_rest%d" % t, acc[:], cols.stop - cols.start, "h_rest%d" % t))
+        for t in range(PACK):
+            scatter(t, entries(1) if t < 2 else slice(0, S // 16), rest[t][:])
             finish(t)
-            for c in range(3):
-                round_rows(nc.scalar.copy, c, t)
-        for c in range(3):
-            weave_pair(nc.scalar.copy, c, 0)
-        scatter(2, slice(0, S // 16), h_full[2][:])
-        finish(2)
-        round_rows(nc.scalar.copy, 0, 2)
-        for c in (1, 2):
-            round_in_place(c, 2)
-        scatter(3, slice(0, S // 16), h_full[3][:])
-        finish(3)
+            if t < 2:
+                for i in range(2):
+                    nc.scalar.copy(low[i][:, t, :], page[t][:, i * 512 : (i + 1) * 512])
+            if t == 1:
+                for c in range(4):
+                    nc.scalar.copy(og[c][:, :, 0:2], low[c // 2][:, :, spans[c % 2]].rearrange("p t c -> p c t"))
+            if t == 2:
+                for c in (0, 1):
+                    round_rows(nc.scalar.copy, c, t)
+            if t >= 2:
+                for c in (2, 3):
+                    round_in_place(c, t)
 
         ow = sb("ow", [P, U], I32)
         osc = sb("osc", [P, U], U8)
         out_words = words_of(out_1)
-        round_rows(nc.vector.tensor_copy, 0, 3)
-        weave_pair(nc.vector.tensor_copy, 0, 1)
-        for c in (1, 2):
-            round_in_place(c, 3)
-        for c in (1, 0, 2):
+        for c in (0, 1):
+            round_rows(nc.vector.tensor_copy, c, 3)
+        for c in (0, 1):
+            weave_pair(c)
+        for c in (0, 2, 1, 3):
             cols = spans[c]
             nc.vector.quantize_mx(ow[:, cols].bitcast(FP8X4), osc[:, cols], og[c][:].rearrange("p c t -> p (c t)"))
             nc.sync.dma_start(out_words[:, cols], ow[:, cols])

@@ -132,7 +132,7 @@ def tile_picked_denseminmodpage_none_po_kernel(tc, x_words, x_scales, w1_words, 
 
         def weave(name, src, func, scale):
             dst = sb(name, [P, WOVEN], BF16)
-            nc.scalar.activation(dst[:].rearrange("p (j t) -> p j t", t=PACK), src[:].rearrange("p t j -> p j t"), func, scale=scale)
+            nc.scalar.activation(dst[:].rearrange("p (c i t) -> p c t i", i=4, t=PACK), src[:].rearrange("p t (c i) -> p c t i", i=4), func, scale=scale)
             return dst
 
         def bounds(h):
@@ -243,7 +243,9 @@ def tile_picked_denseminmodpage_none_po_kernel(tc, x_words, x_scales, w1_words, 
         for c in (0, 2, 1, 3):
             cols = spans[c]
             nc.vector.quantize_mx(ow[:, cols].bitcast(FP8X4), osc[:, cols], og[c][:].rearrange("p c t -> p (c t)"))
-            nc.sync.dma_start(out_words[:, cols], ow[:, cols])
+            if c != 2:
+                done = slice(cols.start, spans[2].stop) if c == 1 else cols
+                nc.sync.dma_start(out_words[:, done], ow[:, done])
         for q in range(4):
             eng = nc.sync if q == 3 else nc.scalar
             eng.dma_start(out_2[0][4 * q : 4 * q + 4, :].bitcast(I32), osc[32 * q : 32 * q + 4, :].bitcast(I32))

from contextlib import ExitStack

import concourse.mybir as mybir

F32 = mybir.dt.float32
BF16 = mybir.dt.bfloat16
I32 = mybir.dt.int32
U32 = mybir.dt.uint32
U16 = mybir.dt.uint16
U8 = mybir.dt.uint8
FP8X4 = mybir.dt.float8_e4m3fn_x4
ALU = mybir.AluOpType
COPY = mybir.ActivationFunctionType.Copy
RELU = mybir.ActivationFunctionType.Relu

P = 128
PACK = 4
K, T, S, H, G, U = 512, 2048, 512, 512, 2048, 1024
HALF = S // 2
LCOLS = HALF // 16
FLOPS = 2 * 2 * K * H * S


def tile_picked_denseminmodpage_none_po_kernel(tc, x_words, x_scales, w1_words, w1_scales, gs, d_words, d_scales, mem, offs, n1, n2, k1, n3, out_0, out_1, out_2):
    nc = tc.nc
    with ExitStack() as ctx:
        keep = ctx.enter_context(tc.tile_pool(name="keep", bufs=1))
        psum = ctx.enter_context(tc.psum_pool(name="psum", bufs=1))

        def sb(name, shape, dtype):
            return keep.tile(shape, dtype, name=name, align_bytes=64)

        def words_of(ap):
            return ap[0].rearrange("p c t -> p (c t)").bitcast(I32)

        def load_list(name, ap):
            tile = keep.tile([P, S // 16], U16, name=name)
            nc.sync.dma_start(tile[:], ap)
            return tile

        def load_scale_rows(queue, tile, ap):
            for q in range(4):
                queue.dma_start(tile[32 * q : 32 * q + 4, :].bitcast(I32), ap[0][4 * q : 4 * q + 4, :].bitcast(I32))

        def deal(dst, src):
            nc.vector.tensor_copy(dst.rearrange("p (t m) -> p t m", t=PACK), src.rearrange("p (m t) -> p t m", t=PACK))

        def deal_words(dst, src):
            nc.vector.tensor_copy(dst.rearrange("p (t m) -> p m t", t=PACK), src.rearrange("p (m t) -> p m t", t=PACK))

        xs_tab = sb("xs_tab", [P, T], U8)
        ws_raw = sb("ws_raw", [P, H], U8)
        ds_tab = sb("ds_tab", [P, G], U8)
        ds_plane = sb("ds_plane", [P, H], U8)
        nc.vector.memset(xs_tab[:].bitcast(I32), 0)
        nc.vector.memset(ws_raw[:].bitcast(I32), 0)
        nc.vector.memset(ds_tab[:].bitcast(I32), 0)
        nc.vector.memset(ds_plane[:].bitcast(I32), 0)

        offs_t = load_list("offs_t", offs)
        ww_raw = sb("ww_raw", [P, H], I32)
        nc.sync.dma_start(ww_raw[:], words_of(w1_words))
        load_scale_rows(nc.sync, xs_tab, x_scales)
        xw_tab = sb("xw_tab", [P, T], I32)
        nc.sync.dma_start(xw_tab[:], words_of(x_words))
        load_scale_rows(nc.sync, ws_raw, w1_scales)
        gain = sb("gain", [P, PACK], F32)
        nc.sync.dma_start(gain[:], gs.rearrange("(p t) o -> p (t o)", t=PACK))
        k1_t = load_list("k1_t", k1)
        nc.sync.dma_start(ds_tab[0:P:8, :].bitcast(I32), d_scales[0].bitcast(I32))
        n1_t = load_list("n1_t", n1)
        n2_t = load_list("n2_t", n2)
        dw_tab = sb("dw_tab", [P, G], I32)
        nc.sync.dma_start(dw_tab[:], words_of(d_words))
        n3_t = load_list("n3_t", n3)
        mem_rows = mem.rearrange("(p t) c -> p t c", t=PACK)
        out_rows = out_0.rearrange("(p t) c -> p t c", t=PACK)
        page = []
        for t in range(PACK):
            page.append(sb("page%d" % t, [P, U], F32))
            nc.sync.dma_start(page[t][:], mem_rows[:, t, :])

        neg_gain = sb("neg_gain", [P, PACK], F32)
        nc.scalar.activation(neg_gain[:], gain[:], COPY, scale=-1.0)

        ww = sb("ww", [P, H], I32)
        deal_words(ww[:], ww_raw[:])
        xs = sb("xs", [P, S], U8)
        nc.vector.tensor_copy(xs[:], xs_tab[:].indirect(offs_t[:]))
        xw = sb("xw", [P, S], I32)
        nc.vector.tensor_copy(xw[:].bitcast(U32), xw_tab[:].bitcast(U32).indirect(offs_t[:]))
        ws = sb("ws", [P, H], U8)
        deal(ws[:], ws_raw[:])
        def half(h):
            return slice(h * HALF, (h + 1) * HALF)

        def entries(h):
            return slice(h * LCOLS, (h + 1) * LCOLS)

        y = [sb("y%d" % h, [P, PACK, HALF], F32) for h in range(2)]
        neg_y, y_acc = [], []
        for t in range(PACK):
            cols = slice(t * P, (t + 1) * P)
            y_acc.append(psum.tile([P, S], F32, name="y_acc%d" % t))
            nc.tensor.matmul_mx(y_acc[t][:], lhsT=ww[:, cols].bitcast(FP8X4), lhsT_scale=ws[:, cols], rhs=xw[:].bitcast(FP8X4), rhs_scale=xs[:], start=True, stop=True)
            neg_y.append(sb("neg_y%d" % t, [P, S], F32))
            nc.scalar.activation(neg_y[t][:], y_acc[t][:], COPY, scale=neg_gain[:, t : t + 1])
            nc.scalar.activation(y[0][:, t, :], y_acc[t][:, half(0)], COPY, scale=gain[:, t : t + 1])
        for t in range(PACK):
            nc.scalar.activation(y[1][:, t, :], y_acc[t][:, half(1)], COPY, scale=gain[:, t : t + 1])

        ds_got = keep.tile([P, H], U8, name="ds_got", tag="ws_raw", align_bytes=64)
        nc.vector.tensor_copy(ds_got[:], ds_tab[:].indirect(k1_t[:]))
        ds_dealt = sb("ds_dealt", [P, H], U8)
        dw_got = sb("dw_got", [P, H], I32)
        nc.vector.tensor_copy(dw_got[:].bitcast(U32), dw_tab[:].bitcast(U32).indirect(k1_t[:]))
        deal(ds_dealt[:], ds_got[:])
        dw = sb("dw", [P, H], I32)
        deal_words(dw[:], dw_got[:])
        for i in range(4):
            src = 8 * i
            nc.sync.dma_start(ds_plane[i:P:32, :].bitcast(I32), ds_dealt[src:P:32, :].bitcast(I32))

        pa = [sb("pa%d" % h, [P, PACK, HALF], F32) for h in range(2)]
        neg_pb = [sb("neg_pb%d" % h, [P, PACK, HALF], F32) for h in range(2)]
        zw = sb("zw", [P, S], I32)
        zs = sb("zs", [P, S], U8)
        WOVEN = HALF * PACK

        def look_up(dst, lst, h, t):
            nc.vector.tensor_tensor(dst[h][:, t, :], neg_y[t][:].indirect(lst[:, entries(h)]), y[h][:, t, :], ALU.add)

        def weave(name, src, func, scale):
            dst = sb(name, [P, WOVEN], BF16)
            nc.scalar.activation(dst[:].rearrange("p (c i t) -> p c t i", i=4, t=PACK), src[:].rearrange("p t (c i) -> p c t i", i=4), func, scale=scale)
            return dst

        def bounds(h):
            a16 = weave("a16_%d" % h, pa[h], COPY, 1.0)
            upper = weave("upper%d" % h, pa[h], RELU, 1.0)
            return a16, upper

        def lower_bound(h, a16):
            lower = sb("lower%d" % h, [P, WOVEN], BF16)
            nc.vector.tensor_scalar_min(lower[:], a16[:], 0.0)
            return lower

        def quantise_z(first, woven, count):
            cols = slice(first, first + count)
            nc.vector.quantize_mx(zw[:, cols].bitcast(FP8X4), zs[:, cols], woven)

        def product(acc, t, cols):
            rows = slice(t * P, (t + 1) * P)
            nc.tensor.matmul_mx(acc, lhsT=dw[:, rows].bitcast(FP8X4), lhsT_scale=ds_plane[:, rows], rhs=zw[:, cols].bitcast(FP8X4), rhs_scale=zs[:, cols], start=True, stop=True)

        def empty(name, acc, width, tag):
            vals = keep.tile([P, width], F32, name=name, tag=tag, align_bytes=64)
            nc.scalar.activation(vals[:], acc, COPY, scale=0.0625)
            return vals

        def scatter(t, cols, src):
            nc.vector.tensor_copy(page[t][:].indirect(n3_t[:, cols]), src)

        spans = [slice(c * 256, (c + 1) * 256) for c in range(4)]
        planes = [sb("planes%d" % c, [P, 2, 256], BF16) for c in range(2)]

        og = [sb("og%d" % c, [P, 256, PACK], BF16) for c in range(4)]
        low = [sb("low%d" % i, [P, 2, 512], BF16) for i in range(2)]

        def finish(t):
            nc.sync.dma_start(out_rows[:, t, :], page[t][:])

        def round_rows(copy, c, t):
            copy(planes[c][:, t - 2, :], page[t][:, spans[c]])

        def weave_pair(c):
            nc.vector.tensor_copy(og[c][:, :, 2:4], planes[c][:].rearrange("p t c -> p c t"))

        def round_in_place(c, t):
            nc.scalar.copy(og[c][:, :, t], page[t][:, spans[c]])

        cap = [sb("cap%d" % h, [P, WOVEN], BF16) for h in range(2)]
        zg = [sb("zg%d" % h, [P, WOVEN], BF16) for h in range(2)]
        for t in range(PACK):
            look_up(pa, n1_t, 0, t)
            look_up(neg_pb, n2_t, 0, t)
        a16, upper = bounds(0)
        b16 = weave("b16_0", neg_pb[0], COPY, -1.0)
        for t in range(PACK):
            look_up(pa, n1_t, 1, t)
        lower0 = lower_bound(0, a16)
        a16, upper1 = bounds(1)
        for t in range(PACK):
            look_up(neg_pb, n2_t, 1, t)
        b16_1 = weave("b16_1", neg_pb[1], COPY, -1.0)
        nc.vector.tensor_tensor(cap[0][:], b16[:], upper[:], ALU.min)
        lower1 = lower_bound(1, a16)
        nc.vector.tensor_tensor(zg[0][:], cap[0][:], lower0[:], ALU.max)
        pieces = (slice(0, WOVEN // 2), slice(WOVEN // 2, WOVEN))
        nc.vector.tensor_tensor(cap[1][:, pieces[0]], b16_1[:, pieces[0]], upper1[:, pieces[0]], ALU.min)
        quantise_z(0, zg[0][:], HALF)
        acc_a = [psum.tile([P, HALF], F32, name="acc_a%d" % t) for t in range(2)]
        for t in range(2):
            product(acc_a[t][:], t, half(0))
        h_a0 = empty("h_a0", acc_a[0][:], HALF, "h_a0")
        nc.vector.tensor_tensor(cap[1][:, pieces[1]], b16_1[:, pieces[1]], upper1[:, pieces[1]], ALU.min)
        for cols in pieces:
            nc.vector.tensor_tensor(zg[1][:, cols], cap[1][:, cols], lower1[:, cols], ALU.max)
        for i, cols in enumerate(pieces):
            quantise_z(HALF + i * HALF // 2, zg[1][:, cols], HALF // 2)
        h_a1 = empty("h_a1", acc_a[1][:], HALF, "cap1")
        scatter(0, entries(0), h_a0[:])
        scatter(1, entries(0), h_a1[:])
        rest = []
        for t in range(PACK):
            cols = half(1) if t < 2 else slice(0, S)
            acc = psum.tile([P, cols.stop - cols.start], F32, name="acc_rest%d" % t, tag="y_acc%d" % t)
            product(acc[:], t, cols)
            rest.append(empty("h_rest%d" % t, acc[:], cols.stop - cols.start, "h_rest%d" % t))
        for t in range(PACK):
            scatter(t, entries(1) if t < 2 else slice(0, S // 16), rest[t][:])
            finish(t)
            if t < 2:
                for i in range(2):
                    nc.scalar.copy(low[i][:, t, :], page[t][:, i * 512 : (i + 1) * 512])
            if t == 1:
                for c in range(4):
                    nc.scalar.copy(og[c][:, :, 0:2], low[c // 2][:, :, spans[c % 2]].rearrange("p t c -> p c t"))
            if t == 2:
                for c in (0, 1):
                    round_rows(nc.scalar.copy, c, t)
            if t >= 2:
                for c in (2, 3):
                    round_in_place(c, t)

        ow = sb("ow", [P, U], I32)
        osc = sb("osc", [P, U], U8)
        out_words = words_of(out_1)
        for c in (0, 1):
            round_rows(nc.vector.tensor_copy, c, 3)
        for c in (0, 1):
            weave_pair(c)
        for c in (0, 2, 1, 3):
            cols = spans[c]
            nc.vector.quantize_mx(ow[:, cols].bitcast(FP8X4), osc[:, cols], og[c][:].rearrange("p c t -> p (c t)"))
            if c != 2:
                done = slice(cols.start, spans[2].stop) if c == 1 else cols
                nc.sync.dma_start(out_words[:, done], ow[:, done])
        for q in range(4):
            eng = nc.sync if q == 3 else nc.scalar
            eng.dma_start(out_2[0][4 * q : 4 * q + 4, :].bitcast(I32), osc[32 * q : 32 * q + 4, :].bitcast(I32))
